import numpy as np, ml_dtypes
CORES = [24,26,29,31,48,50,53,55]
N = 8
TK, LAY = 512, 3
def setup_inputs(rng):
    return {"x": rng.standard_normal((N, 128, TK), dtype=np.float32).astype(ml_dtypes.bfloat16), "w": (rng.standard_normal((N, 128, LAY * 256), dtype=np.float32) / 16).astype(ml_dtypes.bfloat16)}
def setup_inputs_big(rng):
    d = setup_inputs(rng)
    for k in ("x",): d[k] = (d[k].astype(np.float32) * 1048576.0).astype(d[k].dtype)
    return d
def setup_inputs_small(rng):
    d = setup_inputs(rng)
    for k in ("x",): d[k] = (d[k].astype(np.float32) * (1 / 1048576.0)).astype(d[k].dtype)
    return d
def setup_inputs_apart(rng):
    d = setup_inputs(rng)
    f = (10.0 ** rng.permutation(np.linspace(-1.5, 1.5, N))).astype(np.float32).reshape(N, 1, 1)
    for k in ("x",): d[k] = (d[k].astype(np.float32) * f).astype(d[k].dtype)
    return d
def reference(x, w):
    X, W = x.astype(np.float64), w.astype(np.float64)
    h = list(X)
    for l in range(LAY):
        h = [np.maximum(W[r][:, 256 * l:256 * l + 128].T @ h[r] + W[r][:, 256 * l + 128:256 * l + 256].T @ h[r ^ (1 << l)], 0.0) for r in range(N)]
    return {"y": np.stack(h).astype(ml_dtypes.bfloat16)}

@@ -1,0 +1,164 @@
+from concourse.bass import DstId, RemoteDMATransfer
+from concourse.mybir import AluOpType
+
+TK = 512
+KC = 2
+W = TK // KC
+BF, F32 = "bfloat16", "float32"
+
+SCRATCH = {
+    "xs": ("sbuf", [128, TK], BF),
+    "ws": ("sbuf", [128, 768], BF),
+    "xp": ("sbuf", [128, TK], BF),
+    "h1": ("sbuf", [128, TK], BF),
+    "h1p": ("sbuf", [128, TK], BF),
+    "pw": ("sbuf", [128, 256], BF),
+    "ph": ("sbuf", [128, TK], BF),
+    "php": ("sbuf", [128, TK], BF),
+    "h2": ("sbuf", [128, TK], BF),
+    "ph2": ("sbuf", [128, TK], BF),
+    "h2p": ("sbuf", [128, TK], BF),
+    "ys": ("sbuf", [128, TK], BF),
+    "zero": ("sbuf", [128, W], F32),
+}
+for _n in ("a0", "a1", "ap", "a2"):
+    for _k in range(KC):
+        SCRATCH["%s_%d" % (_n, _k)] = ("psum", [128, 512], F32)
+
+SEMAPHORES = ["ldx", "ldw0", "ldw1", "ldw2", "zs", "ax", "apw", "aph", "aphp", "ah1", "ah2", "st", "sent"]
+for _n in ("m0", "m1", "mp", "m2", "r0", "r1", "rp", "r2"):
+    for _k in range(KC):
+        SEMAPHORES.append("%s_%d" % (_n, _k))
+
+
+def rank_program(g, core, T, topo):
+    rank = T.rank_of(core)
+    if rank is None:
+        return
+    cores = T.cores
+    n = len(cores)
+    sem = T.sem
+
+    def carrier(r):
+        dst = cores[r ^ 4]
+        if topo.may_write(cores[r], dst):
+            return r
+        cand = [q for q in range(n) if q != r and topo.chip(cores[q]) == topo.chip(cores[r])
+                and topo.may_write(cores[q], dst) and topo.may_write(cores[q], cores[q ^ 4])]
+        cand.sort(key=lambda q: (topo.die(cores[q]) != topo.die(cores[r]), abs(q - r)))
+        return cand[0]
+
+    def bits(m):
+        return [b for b in range(m.bit_length()) if (m >> b) & 1]
+
+    def to_mask(bs):
+        m = 0
+        for b in bs:
+            m |= 1 << b
+        return m
+
+    on = bits(topo.mask(core, cores[rank ^ 1]))
+    far = bits(topo.mask(core, cores[rank ^ 4]))
+    rest = [b for b in on if b not in far]
+    n_on, n_far, n_rest, n_half = len(on), len(far), len(rest), len(on) // 2
+
+    mine = carrier(rank)
+    clients = [r for r in range(n) if r != rank and carrier(r) == rank]
+    client = clients[0] if clients else None
+    sent = [0]
+
+    def send(dst_rank, out_ap, in_ap, rsem, engs):
+        rid, pid, _ = topo.addr(cores[dst_rank])
+        g.remote_dma(out_ap=out_ap, in_ap=in_ap, remote_sem=rsem, local_sem=sem.sent, pid=pid, routing_id=rid,
+                     dma_engine_mask=to_mask(engs))
+        sent[0] += len(engs)
+
+    def col(k):
+        return slice(k * W, (k + 1) * W)
+
+    def names(stem):
+        return [sem["%s_%d" % (stem, k)] for k in range(KC)]
+
+    def banks(stem):
+        return [T["%s_%d" % (stem, k)] for k in range(KC)]
+
+    def u_term(acc, wt, h, waits):
+        for s, v in waits:
+            g.tensor.wait_ge(s, v)
+        for k in range(KC):
+            g.tensor.matmul(acc[k][:, 0:W], wt, h[:, col(k)], True, False)
+
+    def v_term(acc, wt, h, waits, done):
+        for s, v in waits:
+            g.tensor.wait_ge(s, v)
+        for k in range(KC):
+            g.tensor.matmul(acc[k][:, 0:W], wt, h[:, col(k)], False, True).then_inc(done[k], 1)
+
+    def relu(out, acc, done, ready):
+        for k in range(KC):
+            g.vector.wait_ge(done[k], 1)
+            g.vector.tensor_tensor(out[:, col(k)], acc[k][:, 0:W], T.zero[:], AluOpType.max).then_inc(ready[k], 1)
+
+    def ones(sems):
+        return [(s, 1) for s in sems]
+
+    g.sync.dma_start(T.xs[:], T.x[:]).then_inc(sem.ldx, 16)
+    g.sync.dma_start(T.ws[:, 0:256], T.w[:, 0:256]).then_inc(sem.ldw0, 16)
+    g.scalar.wait_ge(sem.ldx, 16)
+    g.scalar.dma_start(T.ws[:, 256:512], T.w[:, 256:512]).then_inc(sem.ldw1, 16)
+    g.scalar.dma_start(T.ws[:, 512:768], T.w[:, 512:768]).then_inc(sem.ldw2, 16)
+    g.vector.memset(T.zero[:], 0.0).then_inc(sem.zs, 1)
+    g.vector.wait_ge(sem.zs, 1)
+
+    g.wait_ge(sem.ldx, 16)
+    send(rank ^ 1, T.xp[:], T.xs[:], sem.ax, far)
+    if mine != rank:
+        g.wait_ge(sem.ldw1, 16)
+        send(mine, T.pw[:], T.ws[:, 256:512], sem.apw, rest)
+    u_term(banks("a0"), T.ws[:, 0:128], T.xs, [(sem.ldx, 16), (sem.ldw0, 16)])
+    v_term(banks("a0"), T.ws[:, 128:256], T.xp, [(sem.ax, n_far)], names("m0"))
+    relu(T.h1, banks("a0"), names("m0"), names("r0"))
+
+    for s in names("r0"):
+        g.wait_ge(s, 1)
+    if mine != rank:
+        other = carrier(rank ^ 2)
+        trs = []
+        for dst_rank, buf, rsem in ((mine, T.ph, sem.aph), (other, T.php, sem.aphp)):
+            rid, pid, _ = topo.addr(cores[dst_rank])
+            crosses = topo.die(cores[dst_rank]) != topo.die(core)
+            engs = on[0::2] if crosses else on[1::2]
+            trs.append(RemoteDMATransfer(dst_ids=[DstId(rid=rid, pnc=pid)], dma_engine_mask=to_mask(engs),
+                                         remote_sem=rsem, src=T.h1[:], dst=buf[:]))
+            sent[0] += len(engs)
+        g.remote_dma_fused(trs, local_sem=sem.sent)
+        send(rank ^ 2, T.h1p[:], T.h1[:], sem.ah1, on)
+        n_h1 = n_on
+    else:
+        send(rank ^ 2, T.h1p[:], T.h1[:], sem.ah1, far)
+        n_h1 = n_far
+    u_term(banks("a1"), T.ws[:, 256:384], T.h1, ones(names("r0")) + [(sem.ldw1, 16)])
+    v_term(banks("a1"), T.ws[:, 384:512], T.h1p, [(sem.ah1, n_h1)], names("m1"))
+    relu(T.h2, banks("a1"), names("m1"), names("r1"))
+    if client is not None:
+        u_term(banks("ap"), T.pw[:, 0:128], T.ph, [(sem.apw, n_rest), (sem.aph, n_half)])
+        v_term(banks("ap"), T.pw[:, 128:256], T.php, [(sem.aphp, n_half)], names("mp"))
+        relu(T.ph2, banks("ap"), names("mp"), names("rp"))
+
+    if mine == rank:
+        for s in names("r1"):
+            g.wait_ge(s, 1)
+        send(rank ^ 4, T.h2p[:], T.h2[:], sem.ah2, far)
+        if client is not None:
+            for s in names("rp"):
+                g.wait_ge(s, 1)
+            send(client ^ 4, T.h2p[:], T.ph2[:], sem.ah2, far)
+    u_term(banks("a2"), T.ws[:, 512:640], T.h2, ones(names("r1")) + [(sem.ldw2, 16)])
+    v_term(banks("a2"), T.ws[:, 640:768], T.h2p, [(sem.ah2, n_far)], names("m2"))
+    relu(T.ys, banks("a2"), names("m2"), names("r2"))
+
+    for s in names("r2"):
+        g.sync.wait_ge(s, 1)
+    g.sync.dma_start(T.y[:], T.ys[:]).then_inc(sem.st, 16)
+    g.sync.wait_ge(sem.st, 16)
+    g.wait_ge(sem.sent, sent[0])

@@ -4,6 +4,9 @@ from concourse.mybir import AluOpType
 TK = 512
 KC = 2
 W = TK // KC
+X_ALL = False
+C1_ALL = False
+S0, S1, S2 = 1, 2, 2
 BF, F32 = "bfloat16", "float32"
 
 SCRATCH = {
@@ -25,8 +28,8 @@ for _n in ("a0", "a1", "ap", "a2"):
     for _k in range(KC):
         SCRATCH["%s_%d" % (_n, _k)] = ("psum", [128, 512], F32)
 
-SEMAPHORES = ["ldx", "ldw0", "ldw1", "ldw2", "zs", "ax", "apw", "aph", "aphp", "ah1", "ah2", "st", "sent"]
-for _n in ("m0", "m1", "mp", "m2", "r0", "r1", "rp", "r2"):
+SEMAPHORES = ["ldx", "ldw0", "ldw1", "ldw2", "zs", "apw", "sent"]
+for _n in ("ax", "aph", "aphp", "ah1", "ah2", "m0", "m1", "mp", "m2", "r0", "r1", "rp", "r2", "st"):
     for _k in range(KC):
         SEMAPHORES.append("%s_%d" % (_n, _k))
 
@@ -60,18 +63,13 @@ def rank_program(g, core, T, topo):
     on = bits(topo.mask(core, cores[rank ^ 1]))
     far = bits(topo.mask(core, cores[rank ^ 4]))
     rest = [b for b in on if b not in far]
-    n_on, n_far, n_rest, n_half = len(on), len(far), len(rest), len(on) // 2
+    e_x = on if X_ALL else far
+    e_c1 = on if C1_ALL else far
 
     mine = carrier(rank)
     clients = [r for r in range(n) if r != rank and carrier(r) == rank]
     client = clients[0] if clients else None
     sent = [0]
-
-    def send(dst_rank, out_ap, in_ap, rsem, engs):
-        rid, pid, _ = topo.addr(cores[dst_rank])
-        g.remote_dma(out_ap=out_ap, in_ap=in_ap, remote_sem=rsem, local_sem=sem.sent, pid=pid, routing_id=rid,
-                     dma_engine_mask=to_mask(engs))
-        sent[0] += len(engs)
 
     def col(k):
         return slice(k * W, (k + 1) * W)
@@ -82,20 +80,42 @@ def rank_program(g, core, T, topo):
     def banks(stem):
         return [T["%s_%d" % (stem, k)] for k in range(KC)]
 
-    def u_term(acc, wt, h, waits):
+    def piece(j, s):
+        return slice(j * (TK // s), (j + 1) * (TK // s))
+
+    def send(s, ready, dests, js=None):
+        for j in (range(s) if js is None else js):
+            for k in range(KC):
+                if k * s // KC == j and ready is not None:
+                    g.wait_ge(ready[k], 1)
+            trs = []
+            for dst_rank, buf, src, arr, engs in dests:
+                rid, pid, _ = topo.addr(cores[dst_rank])
+                sent[0] += len(engs)
+                if len(dests) == 1:
+                    g.remote_dma(out_ap=buf[:, piece(j, s)], in_ap=src[:, piece(j, s)], remote_sem=arr[j],
+                                 local_sem=sem.sent, pid=pid, routing_id=rid, dma_engine_mask=to_mask(engs))
+                else:
+                    trs.append(RemoteDMATransfer(dst_ids=[DstId(rid=rid, pnc=pid)], dma_engine_mask=to_mask(engs),
+                                                 remote_sem=arr[j], src=src[:, piece(j, s)],
+                                                 dst=buf[:, piece(j, s)]))
+            if trs:
+                g.remote_dma_fused(trs, local_sem=sem.sent)
+
+    def u_term(acc, wt, h, waits, ks=range(KC)):
         for s, v in waits:
             g.tensor.wait_ge(s, v)
-        for k in range(KC):
+        for k in ks:
             g.tensor.matmul(acc[k][:, 0:W], wt, h[:, col(k)], True, False)
 
-    def v_term(acc, wt, h, waits, done):
-        for s, v in waits:
-            g.tensor.wait_ge(s, v)
-        for k in range(KC):
+    def v_term(acc, wt, h, arr, s, count, done, ks=range(KC)):
+        for k in ks:
+            if k * s // KC != (k - 1) * s // KC or k == ks[0]:
+                g.tensor.wait_ge(arr[k * s // KC], count)
             g.tensor.matmul(acc[k][:, 0:W], wt, h[:, col(k)], False, True).then_inc(done[k], 1)
 
-    def relu(out, acc, done, ready):
-        for k in range(KC):
+    def relu(out, acc, done, ready, ks=range(KC)):
+        for k in ks:
             g.vector.wait_ge(done[k], 1)
             g.vector.tensor_tensor(out[:, col(k)], acc[k][:, 0:W], T.zero[:], AluOpType.max).then_inc(ready[k], 1)
 
@@ -111,54 +131,50 @@ def rank_program(g, core, T, topo):
     g.vector.wait_ge(sem.zs, 1)
 
     g.wait_ge(sem.ldx, 16)
-    send(rank ^ 1, T.xp[:], T.xs[:], sem.ax, far)
+    send(S0, None, [(rank ^ 1, T.xp, T.xs, names("ax"), e_x)])
     if mine != rank:
         g.wait_ge(sem.ldw1, 16)
-        send(mine, T.pw[:], T.ws[:, 256:512], sem.apw, rest)
+        rid, pid, _ = topo.addr(cores[mine])
+        g.remote_dma(out_ap=T.pw[:], in_ap=T.ws[:, 256:512], remote_sem=sem.apw, local_sem=sem.sent, pid=pid,
+                     routing_id=rid, dma_engine_mask=to_mask(rest))
+        sent[0] += len(rest)
     u_term(banks("a0"), T.ws[:, 0:128], T.xs, [(sem.ldx, 16), (sem.ldw0, 16)])
-    v_term(banks("a0"), T.ws[:, 128:256], T.xp, [(sem.ax, n_far)], names("m0"))
+    v_term(banks("a0"), T.ws[:, 128:256], T.xp, names("ax"), S0, len(e_x), names("m0"))
     relu(T.h1, banks("a0"), names("m0"), names("r0"))
 
-    for s in names("r0"):
-        g.wait_ge(s, 1)
     if mine != rank:
-        other = carrier(rank ^ 2)
-        trs = []
-        for dst_rank, buf, rsem in ((mine, T.ph, sem.aph), (other, T.php, sem.aphp)):
-            rid, pid, _ = topo.addr(cores[dst_rank])
+        dests = []
+        for dst_rank, buf, arr in ((mine, T.ph, names("aph")), (carrier(rank ^ 2), T.php, names("aphp"))):
             crosses = topo.die(cores[dst_rank]) != topo.die(core)
-            engs = on[0::2] if crosses else on[1::2]
-            trs.append(RemoteDMATransfer(dst_ids=[DstId(rid=rid, pnc=pid)], dma_engine_mask=to_mask(engs),
-                                         remote_sem=rsem, src=T.h1[:], dst=buf[:]))
-            sent[0] += len(engs)
-        g.remote_dma_fused(trs, local_sem=sem.sent)
-        send(rank ^ 2, T.h1p[:], T.h1[:], sem.ah1, on)
-        n_h1 = n_on
+            dests.append((dst_rank, buf, T.h1, arr, on[0::2] if crosses else on[1::2]))
+        send(S1, names("r0"), dests)
+        send(1, None, [(rank ^ 2, T.h1p, T.h1, names("ah1"), on)])
+        s_h1, n_h1 = 1, len(on)
     else:
-        send(rank ^ 2, T.h1p[:], T.h1[:], sem.ah1, far)
-        n_h1 = n_far
+        send(S1, names("r0"), [(rank ^ 2, T.h1p, T.h1, names("ah1"), e_c1)])
+        s_h1, n_h1 = S1, len(e_c1)
     u_term(banks("a1"), T.ws[:, 256:384], T.h1, ones(names("r0")) + [(sem.ldw1, 16)])
-    v_term(banks("a1"), T.ws[:, 384:512], T.h1p, [(sem.ah1, n_h1)], names("m1"))
-    relu(T.h2, banks("a1"), names("m1"), names("r1"))
-    if client is not None:
-        u_term(banks("ap"), T.pw[:, 0:128], T.ph, [(sem.apw, n_rest), (sem.aph, n_half)])
-        v_term(banks("ap"), T.pw[:, 128:256], T.php, [(sem.aphp, n_half)], names("mp"))
-        relu(T.ph2, banks("ap"), names("mp"), names("rp"))
+    groups = [[k] for k in range(KC)] if S1 > 1 else [list(range(KC))]
+    for ks in groups:
+        v_term(banks("a1"), T.ws[:, 384:512], T.h1p, names("ah1"), s_h1, n_h1, names("m1"), ks)
+        relu(T.h2, banks("a1"), names("m1"), names("r1"), ks)
+        if client is not None:
+            u_term(banks("ap"), T.pw[:, 0:128], T.ph,
+                   [(sem.apw, len(rest)), (names("aph")[ks[0] * S1 // KC], len(on) // 2)], ks)
+            v_term(banks("ap"), T.pw[:, 128:256], T.php, names("aphp"), S1, len(on) // 2, names("mp"), ks)
+            relu(T.ph2, banks("ap"), names("mp"), names("rp"), ks)
 
     if mine == rank:
-        for s in names("r1"):
-            g.wait_ge(s, 1)
-        send(rank ^ 4, T.h2p[:], T.h2[:], sem.ah2, far)
-        if client is not None:
-            for s in names("rp"):
-                g.wait_ge(s, 1)
-            send(client ^ 4, T.h2p[:], T.ph2[:], sem.ah2, far)
+        for js in ([[j] for j in range(S2)] if S1 > 1 else [list(range(S2))]):
+            send(S2, names("r1"), [(rank ^ 4, T.h2p, T.h2, names("ah2"), far)], js)
+            if client is not None:
+                send(S2, names("rp"), [(client ^ 4, T.h2p, T.ph2, names("ah2"), far)], js)
     u_term(banks("a2"), T.ws[:, 512:640], T.h2, ones(names("r1")) + [(sem.ldw2, 16)])
-    v_term(banks("a2"), T.ws[:, 640:768], T.h2p, [(sem.ah2, n_far)], names("m2"))
+    v_term(banks("a2"), T.ws[:, 640:768], T.h2p, names("ah2"), S2, len(far), names("m2"))
     relu(T.ys, banks("a2"), names("m2"), names("r2"))
 
-    for s in names("r2"):
-        g.sync.wait_ge(s, 1)
-    g.sync.dma_start(T.y[:], T.ys[:]).then_inc(sem.st, 16)
-    g.sync.wait_ge(sem.st, 16)
+    for k, q in zip(range(KC), (g.sync, g.scalar)):
+        q.wait_ge(names("r2")[k], 1)
+        q.dma_start(T.y[:, col(k)], T.ys[:, col(k)]).then_inc(names("st")[k], 16)
+        q.wait_ge(names("st")[k], 16)
     g.wait_ge(sem.sent, sent[0])

@@ -2,11 +2,9 @@ from concourse.bass import DstId, RemoteDMATransfer
 from concourse.mybir import AluOpType
 
 TK = 512
-KC = 2
+KC = 4
 W = TK // KC
-X_ALL = False
-C1_ALL = False
-S0, S1, S2 = 1, 2, 2
+NP = 2
 BF, F32 = "bfloat16", "float32"
 
 SCRATCH = {
@@ -24,12 +22,14 @@ SCRATCH = {
     "ys": ("sbuf", [128, TK], BF),
     "zero": ("sbuf", [128, W], F32),
 }
-for _n in ("a0", "a1", "ap", "a2"):
-    for _k in range(KC):
-        SCRATCH["%s_%d" % (_n, _k)] = ("psum", [128, 512], F32)
+for _k in range(2 * KC):
+    SCRATCH["bank_%d" % _k] = ("psum", [128, 512], F32)
 
-SEMAPHORES = ["ldx", "ldw0", "ldw1", "ldw2", "zs", "apw", "sent"]
-for _n in ("ax", "aph", "aphp", "ah1", "ah2", "m0", "m1", "mp", "m2", "r0", "r1", "rp", "r2", "st"):
+SEMAPHORES = ["ldw0", "ldw12", "zs", "apw", "sent"]
+for _n in ("ldx", "ax", "aph", "aphp", "ah1", "ah2", "st"):
+    for _k in range(NP):
+        SEMAPHORES.append("%s_%d" % (_n, _k))
+for _n in ("m0", "m1", "mp", "m2", "r0", "r1", "rp", "r2"):
     for _k in range(KC):
         SEMAPHORES.append("%s_%d" % (_n, _k))
 
@@ -63,8 +63,6 @@ def rank_program(g, core, T, topo):
     on = bits(topo.mask(core, cores[rank ^ 1]))
     far = bits(topo.mask(core, cores[rank ^ 4]))
     rest = [b for b in on if b not in far]
-    e_x = on if X_ALL else far
-    e_c1 = on if C1_ALL else far
 
     mine = carrier(rank)
     clients = [r for r in range(n) if r != rank and carrier(r) == rank]
@@ -74,107 +72,113 @@ def rank_program(g, core, T, topo):
     def col(k):
         return slice(k * W, (k + 1) * W)
 
+    def half(j):
+        return slice(j * (TK // NP), (j + 1) * (TK // NP))
+
+    def quarters(j):
+        return [k for k in range(KC) if k * NP // KC == j]
+
+    def halves(stem):
+        return [sem["%s_%d" % (stem, j)] for j in range(NP)]
+
     def names(stem):
         return [sem["%s_%d" % (stem, k)] for k in range(KC)]
 
-    def banks(stem):
-        return [T["%s_%d" % (stem, k)] for k in range(KC)]
+    def banks(first):
+        return [T["bank_%d" % (first + k)] for k in range(KC)]
 
-    def piece(j, s):
-        return slice(j * (TK // s), (j + 1) * (TK // s))
+    low, high = banks(0), banks(KC)
 
-    def send(s, ready, dests, js=None):
-        for j in (range(s) if js is None else js):
-            for k in range(KC):
-                if k * s // KC == j and ready is not None:
-                    g.wait_ge(ready[k], 1)
-            trs = []
-            for dst_rank, buf, src, arr, engs in dests:
-                rid, pid, _ = topo.addr(cores[dst_rank])
-                sent[0] += len(engs)
-                if len(dests) == 1:
-                    g.remote_dma(out_ap=buf[:, piece(j, s)], in_ap=src[:, piece(j, s)], remote_sem=arr[j],
-                                 local_sem=sem.sent, pid=pid, routing_id=rid, dma_engine_mask=to_mask(engs))
-                else:
-                    trs.append(RemoteDMATransfer(dst_ids=[DstId(rid=rid, pnc=pid)], dma_engine_mask=to_mask(engs),
-                                                 remote_sem=arr[j], src=src[:, piece(j, s)],
-                                                 dst=buf[:, piece(j, s)]))
-            if trs:
-                g.remote_dma_fused(trs, local_sem=sem.sent)
+    def send(j, waits, dests):
+        for s, v in waits:
+            g.wait_ge(s, v)
+        cs = slice(0, TK) if j is None else half(j)
+        trs = []
+        for dst_rank, buf, src, arr, engs in dests:
+            rid, pid, _ = topo.addr(cores[dst_rank])
+            sent[0] += len(engs)
+            if len(dests) == 1:
+                g.remote_dma(out_ap=buf[:, cs], in_ap=src[:, cs], remote_sem=arr, local_sem=sem.sent, pid=pid,
+                             routing_id=rid, dma_engine_mask=to_mask(engs))
+            else:
+                trs.append(RemoteDMATransfer(dst_ids=[DstId(rid=rid, pnc=pid)], dma_engine_mask=to_mask(engs),
+                                             remote_sem=arr, src=src[:, cs], dst=buf[:, cs]))
+        if trs:
+            g.remote_dma_fused(trs, local_sem=sem.sent)
 
-    def u_term(acc, wt, h, waits, ks=range(KC)):
+    def product(acc, wt, h, waits, ks, first, done=None):
         for s, v in waits:
             g.tensor.wait_ge(s, v)
         for k in ks:
-            g.tensor.matmul(acc[k][:, 0:W], wt, h[:, col(k)], True, False)
+            mm = g.tensor.matmul(acc[k][:, 0:W], wt, h[:, col(k)], first, done is not None)
+            if done is not None:
+                mm.then_inc(done[k], 1)
 
-    def v_term(acc, wt, h, arr, s, count, done, ks=range(KC)):
-        for k in ks:
-            if k * s // KC != (k - 1) * s // KC or k == ks[0]:
-                g.tensor.wait_ge(arr[k * s // KC], count)
-            g.tensor.matmul(acc[k][:, 0:W], wt, h[:, col(k)], False, True).then_inc(done[k], 1)
-
-    def relu(out, acc, done, ready, ks=range(KC)):
+    def relu(out, acc, done, ready, ks):
         for k in ks:
             g.vector.wait_ge(done[k], 1)
             g.vector.tensor_tensor(out[:, col(k)], acc[k][:, 0:W], T.zero[:], AluOpType.max).then_inc(ready[k], 1)
 
-    def ones(sems):
-        return [(s, 1) for s in sems]
+    def ones(sems, ks=range(KC)):
+        return [(sems[k], 1) for k in ks]
 
-    g.sync.dma_start(T.xs[:], T.x[:]).then_inc(sem.ldx, 16)
+    every = list(range(KC))
+
+    for j in range(NP):
+        g.sync.dma_start(T.xs[:, half(j)], T.x[:, half(j)]).then_inc(halves("ldx")[j], 16)
     g.sync.dma_start(T.ws[:, 0:256], T.w[:, 0:256]).then_inc(sem.ldw0, 16)
-    g.scalar.wait_ge(sem.ldx, 16)
-    g.scalar.dma_start(T.ws[:, 256:512], T.w[:, 256:512]).then_inc(sem.ldw1, 16)
-    g.scalar.dma_start(T.ws[:, 512:768], T.w[:, 512:768]).then_inc(sem.ldw2, 16)
+    g.sync.dma_start(T.ws[:, 256:768], T.w[:, 256:768]).then_inc(sem.ldw12, 16)
     g.vector.memset(T.zero[:], 0.0).then_inc(sem.zs, 1)
     g.vector.wait_ge(sem.zs, 1)
 
-    g.wait_ge(sem.ldx, 16)
-    send(S0, None, [(rank ^ 1, T.xp, T.xs, names("ax"), e_x)])
+    for j in range(NP):
+        send(j, [(halves("ldx")[j], 16)], [(rank ^ 1, T.xp, T.xs, halves("ax")[j], far)])
     if mine != rank:
-        g.wait_ge(sem.ldw1, 16)
+        g.wait_ge(sem.ldw12, 16)
         rid, pid, _ = topo.addr(cores[mine])
         g.remote_dma(out_ap=T.pw[:], in_ap=T.ws[:, 256:512], remote_sem=sem.apw, local_sem=sem.sent, pid=pid,
                      routing_id=rid, dma_engine_mask=to_mask(rest))
         sent[0] += len(rest)
-    u_term(banks("a0"), T.ws[:, 0:128], T.xs, [(sem.ldx, 16), (sem.ldw0, 16)])
-    v_term(banks("a0"), T.ws[:, 128:256], T.xp, names("ax"), S0, len(e_x), names("m0"))
-    relu(T.h1, banks("a0"), names("m0"), names("r0"))
+    product(low, T.ws[:, 0:128], T.xs, [(s, 16) for s in halves("ldx")] + [(sem.ldw0, 16)], every, True)
+    for j in range(NP):
+        product(low, T.ws[:, 128:256], T.xp, [(halves("ax")[j], len(far))], quarters(j), False, names("m0"))
+    relu(T.h1, low, names("m0"), names("r0"), every)
 
     if mine != rank:
-        dests = []
-        for dst_rank, buf, arr in ((mine, T.ph, names("aph")), (carrier(rank ^ 2), T.php, names("aphp"))):
-            crosses = topo.die(cores[dst_rank]) != topo.die(core)
-            dests.append((dst_rank, buf, T.h1, arr, on[0::2] if crosses else on[1::2]))
-        send(S1, names("r0"), dests)
-        send(1, None, [(rank ^ 2, T.h1p, T.h1, names("ah1"), on)])
-        s_h1, n_h1 = 1, len(on)
+        for j in range(NP):
+            dests = []
+            for dst_rank, buf, arr in ((mine, T.ph, halves("aph")), (carrier(rank ^ 2), T.php, halves("aphp"))):
+                crosses = topo.die(cores[dst_rank]) != topo.die(core)
+                dests.append((dst_rank, buf, T.h1, arr[j], on[0::2] if crosses else on[1::2]))
+            send(j, ones(names("r0"), quarters(j)), dests)
+        send(None, [], [(rank ^ 2, T.h1p, T.h1, halves("ah1")[0], on)])
     else:
-        send(S1, names("r0"), [(rank ^ 2, T.h1p, T.h1, names("ah1"), e_c1)])
-        s_h1, n_h1 = S1, len(e_c1)
-    u_term(banks("a1"), T.ws[:, 256:384], T.h1, ones(names("r0")) + [(sem.ldw1, 16)])
-    groups = [[k] for k in range(KC)] if S1 > 1 else [list(range(KC))]
-    for ks in groups:
-        v_term(banks("a1"), T.ws[:, 384:512], T.h1p, names("ah1"), s_h1, n_h1, names("m1"), ks)
-        relu(T.h2, banks("a1"), names("m1"), names("r1"), ks)
+        for j in range(NP):
+            send(j, ones(names("r0"), quarters(j)), [(rank ^ 2, T.h1p, T.h1, halves("ah1")[j], far)])
+    product(high, T.ws[:, 256:384], T.h1, ones(names("r0")) + [(sem.ldw12, 16)], every, True)
+    for j in range(NP):
+        landed = (halves("ah1")[0], len(on)) if mine != rank else (halves("ah1")[j], len(far))
+        product(high, T.ws[:, 384:512], T.h1p, [landed], quarters(j), False, names("m1"))
+        relu(T.h2, high, names("m1"), names("r1"), quarters(j))
         if client is not None:
-            u_term(banks("ap"), T.pw[:, 0:128], T.ph,
-                   [(sem.apw, len(rest)), (names("aph")[ks[0] * S1 // KC], len(on) // 2)], ks)
-            v_term(banks("ap"), T.pw[:, 128:256], T.php, names("aphp"), S1, len(on) // 2, names("mp"), ks)
-            relu(T.ph2, banks("ap"), names("mp"), names("rp"), ks)
+            for k in quarters(j):
+                product(low, T.pw[:, 0:128], T.ph, [(sem.apw, len(rest)), (halves("aph")[j], len(on) // 2)], [k], True)
+                product(low, T.pw[:, 128:256], T.php, [(halves("aphp")[j], len(on) // 2)], [k], False, names("mp"))
+            relu(T.ph2, low, names("mp"), names("rp"), quarters(j))
 
     if mine == rank:
-        for js in ([[j] for j in range(S2)] if S1 > 1 else [list(range(S2))]):
-            send(S2, names("r1"), [(rank ^ 4, T.h2p, T.h2, names("ah2"), far)], js)
+        for j in range(NP):
+            send(j, ones(names("r1"), quarters(j)), [(rank ^ 4, T.h2p, T.h2, halves("ah2")[j], far)])
             if client is not None:
-                send(S2, names("rp"), [(client ^ 4, T.h2p, T.ph2, names("ah2"), far)], js)
-    u_term(banks("a2"), T.ws[:, 512:640], T.h2, ones(names("r1")) + [(sem.ldw2, 16)])
-    v_term(banks("a2"), T.ws[:, 640:768], T.h2p, names("ah2"), S2, len(far), names("m2"))
-    relu(T.ys, banks("a2"), names("m2"), names("r2"))
+                send(j, ones(names("rp"), quarters(j)), [(client ^ 4, T.h2p, T.ph2, halves("ah2")[j], far)])
+    product(high, T.ws[:, 512:640], T.h2, ones(names("r1")) + [(sem.ldw12, 16)], every, True)
+    for j in range(NP):
+        product(high, T.ws[:, 640:768], T.h2p, [(halves("ah2")[j], len(far))], quarters(j), False, names("m2"))
+    relu(T.ys, high, names("m2"), names("r2"), every)
 
-    for k, q in zip(range(KC), (g.sync, g.scalar)):
-        q.wait_ge(names("r2")[k], 1)
-        q.dma_start(T.y[:, col(k)], T.ys[:, col(k)]).then_inc(names("st")[k], 16)
-        q.wait_ge(names("st")[k], 16)
+    for j, q in zip(range(NP), (g.sync, g.scalar)):
+        for s, v in ones(names("r2"), quarters(j)):
+            q.wait_ge(s, v)
+        q.dma_start(T.y[:, half(j)], T.ys[:, half(j)]).then_inc(halves("st")[j], 16)
+        q.wait_ge(halves("st")[j], 16)
     g.wait_ge(sem.sent, sent[0])

@@ -1,10 +1,11 @@
 from concourse.bass import DstId, RemoteDMATransfer
 from concourse.mybir import AluOpType
 
+NCORES = 64
 TK = 512
 KC = 4
 W = TK // KC
-NP = 2
+PIECES = ((0,), (1,), (2, 3))
 BF, F32 = "bfloat16", "float32"
 
 SCRATCH = {
@@ -25,19 +26,14 @@ SCRATCH = {
 for _k in range(2 * KC):
     SCRATCH["bank_%d" % _k] = ("psum", [128, 512], F32)
 
-SEMAPHORES = ["ldw0", "ldw12", "zs", "apw", "sent"]
-for _n in ("ldx", "ax", "aph", "aphp", "ah1", "ah2", "st"):
-    for _k in range(NP):
-        SEMAPHORES.append("%s_%d" % (_n, _k))
-for _n in ("m0", "m1", "mp", "m2", "r0", "r1", "rp", "r2"):
+SEMAPHORES = ["ldw0", "ldw1", "ldw2", "zs", "apw", "sent"]
+for _n in ("ldx", "ax", "aph", "aphp", "ah1", "ah2", "st", "m0", "m1", "mp", "m2", "r0", "r1", "rp", "r2"):
     for _k in range(KC):
         SEMAPHORES.append("%s_%d" % (_n, _k))
 
 
 def rank_program(g, core, T, topo):
     rank = T.rank_of(core)
-    if rank is None:
-        return
     cores = T.cores
     n = len(cores)
     sem = T.sem
@@ -51,6 +47,19 @@ def rank_program(g, core, T, topo):
         cand.sort(key=lambda q: (topo.die(cores[q]) != topo.die(cores[r]), abs(q - r)))
         return cand[0]
 
+    def helper(r):
+        cand = [c for c in range(NCORES) if c not in cores and topo.chip(c) == topo.chip(cores[r])
+                and topo.may_write(c, cores[r ^ 4])]
+        cand.sort(key=lambda c: (topo.die(c) != topo.die(cores[r]), c))
+        return cand[0]
+
+    served = None
+    if rank is None:
+        mineq = [r for r in range(n) if carrier(r) != r and helper(r) == core]
+        if not mineq:
+            return
+        served = mineq[0]
+
     def bits(m):
         return [b for b in range(m.bit_length()) if (m >> b) & 1]
 
@@ -60,26 +69,17 @@ def rank_program(g, core, T, topo):
             m |= 1 << b
         return m
 
-    on = bits(topo.mask(core, cores[rank ^ 1]))
-    far = bits(topo.mask(core, cores[rank ^ 4]))
+    base = served if rank is None else rank
+    on = bits(topo.mask(core, cores[base] if rank is None else cores[base ^ 1]))
+    far = bits(topo.mask(core, cores[base ^ 4]))
     rest = [b for b in on if b not in far]
-
-    mine = carrier(rank)
-    clients = [r for r in range(n) if r != rank and carrier(r) == rank]
-    client = clients[0] if clients else None
     sent = [0]
 
     def col(k):
         return slice(k * W, (k + 1) * W)
 
-    def half(j):
-        return slice(j * (TK // NP), (j + 1) * (TK // NP))
-
-    def quarters(j):
-        return [k for k in range(KC) if k * NP // KC == j]
-
-    def halves(stem):
-        return [sem["%s_%d" % (stem, j)] for j in range(NP)]
+    def span(ks):
+        return slice(ks[0] * W, (ks[-1] + 1) * W)
 
     def names(stem):
         return [sem["%s_%d" % (stem, k)] for k in range(KC)]
@@ -89,22 +89,31 @@ def rank_program(g, core, T, topo):
 
     low, high = banks(0), banks(KC)
 
-    def send(j, waits, dests):
+    def write(waits, dests):
         for s, v in waits:
             g.wait_ge(s, v)
-        cs = slice(0, TK) if j is None else half(j)
         trs = []
-        for dst_rank, buf, src, arr, engs in dests:
-            rid, pid, _ = topo.addr(cores[dst_rank])
+        for dst, out, src, arr, engs in dests:
+            rid, pid, _ = topo.addr(dst)
             sent[0] += len(engs)
             if len(dests) == 1:
-                g.remote_dma(out_ap=buf[:, cs], in_ap=src[:, cs], remote_sem=arr, local_sem=sem.sent, pid=pid,
+                g.remote_dma(out_ap=out, in_ap=src, remote_sem=arr, local_sem=sem.sent, pid=pid,
                              routing_id=rid, dma_engine_mask=to_mask(engs))
             else:
                 trs.append(RemoteDMATransfer(dst_ids=[DstId(rid=rid, pnc=pid)], dma_engine_mask=to_mask(engs),
-                                             remote_sem=arr, src=src[:, cs], dst=buf[:, cs]))
+                                             remote_sem=arr, src=src, dst=out))
         if trs:
             g.remote_dma_fused(trs, local_sem=sem.sent)
+
+    def deal(dsts):
+        cross = [d for d in dsts if topo.die(d) != topo.die(core)]
+        stay = [d for d in dsts if d not in cross]
+        pools = ((cross, on[0::2]), (stay, on[1::2])) if len(cross) == len(stay) else ((dsts, on),)
+        out = {}
+        for grp, pool in pools:
+            for i, d in enumerate(grp):
+                out[d] = pool[i::len(grp)]
+        return out
 
     def product(acc, wt, h, waits, ks, first, done=None):
         for s, v in waits:
@@ -122,63 +131,83 @@ def rank_program(g, core, T, topo):
     def ones(sems, ks=range(KC)):
         return [(sems[k], 1) for k in ks]
 
-    every = list(range(KC))
+    def second_layer1(k, npw, cnt):
+        product(low, T.pw[:, 0:128], T.ph, [(sem.apw, npw), (names("aph")[k], cnt)], [k], True)
+        product(low, T.pw[:, 128:256], T.php, [(names("aphp")[k], cnt)], [k], False, names("mp"))
+        relu(T.ph2, low, names("mp"), names("rp"), [k])
 
-    for j in range(NP):
-        g.sync.dma_start(T.xs[:, half(j)], T.x[:, half(j)]).then_inc(halves("ldx")[j], 16)
-    g.sync.dma_start(T.ws[:, 0:256], T.w[:, 0:256]).then_inc(sem.ldw0, 16)
-    g.sync.dma_start(T.ws[:, 256:768], T.w[:, 256:768]).then_inc(sem.ldw12, 16)
+    every = list(range(KC))
+    alone = [p[0] for p in PIECES if len(p) == 1]
+    k_help, k_carr = PIECES[-1]
     g.vector.memset(T.zero[:], 0.0).then_inc(sem.zs, 1)
     g.vector.wait_ge(sem.zs, 1)
 
-    for j in range(NP):
-        send(j, [(halves("ldx")[j], 16)], [(rank ^ 1, T.xp, T.xs, halves("ax")[j], far)])
+    if rank is None:
+        write([(sem.apw, len(rest))], [(cores[carrier(served)], T.pw[:], T.pw[:], sem.apw, far)])
+        for k in alone + [k_help]:
+            second_layer1(k, len(rest), len(on) // 2 if k in alone else len(on) // 4)
+            write([(names("rp")[k], 1)], [(cores[served ^ 4], T.h2p[:, col(k)], T.ph2[:, col(k)], names("ah2")[k], far)])
+        g.wait_ge(sem.sent, sent[0])
+        return
+
+    mine = carrier(rank)
+    clients = [r for r in range(n) if r != rank and carrier(r) == rank]
+    client = clients[0] if clients else None
+    npc = len(PIECES)
+
+    for j, ks in enumerate(PIECES):
+        g.sync.dma_start(T.xs[:, span(ks)], T.x[:, span(ks)]).then_inc(names("ldx")[j], 16)
+    for l in ((1, 0, 2) if mine != rank else (0, 1, 2)):
+        g.sync.dma_start(T.ws[:, 256 * l:256 * l + 256], T.w[:, 256 * l:256 * l + 256]).then_inc(sem["ldw%d" % l], 16)
+
+    for j, ks in enumerate(PIECES):
+        write([(names("ldx")[j], 16)], [(cores[rank ^ 1], T.xp[:, span(ks)], T.xs[:, span(ks)], names("ax")[j], far)])
     if mine != rank:
-        g.wait_ge(sem.ldw12, 16)
-        rid, pid, _ = topo.addr(cores[mine])
-        g.remote_dma(out_ap=T.pw[:], in_ap=T.ws[:, 256:512], remote_sem=sem.apw, local_sem=sem.sent, pid=pid,
-                     routing_id=rid, dma_engine_mask=to_mask(rest))
-        sent[0] += len(rest)
-    product(low, T.ws[:, 0:128], T.xs, [(s, 16) for s in halves("ldx")] + [(sem.ldw0, 16)], every, True)
-    for j in range(NP):
-        product(low, T.ws[:, 128:256], T.xp, [(halves("ax")[j], len(far))], quarters(j), False, names("m0"))
+        write([(sem.ldw1, 16)], [(helper(rank), T.pw[:], T.ws[:, 256:512], sem.apw, rest)])
+    product(low, T.ws[:, 0:128], T.xs, [(names("ldx")[j], 16) for j in range(npc)] + [(sem.ldw0, 16)], every, True)
+    for j, ks in enumerate(PIECES):
+        product(low, T.ws[:, 128:256], T.xp, [(names("ax")[j], len(far))], ks, False, names("m0"))
     relu(T.h1, low, names("m0"), names("r0"), every)
 
     if mine != rank:
-        for j in range(NP):
-            dests = []
-            for dst_rank, buf, arr in ((mine, T.ph, halves("aph")), (carrier(rank ^ 2), T.php, halves("aphp"))):
-                crosses = topo.die(cores[dst_rank]) != topo.die(core)
-                dests.append((dst_rank, buf, T.h1, arr[j], on[0::2] if crosses else on[1::2]))
-            send(j, ones(names("r0"), quarters(j)), dests)
-        send(None, [], [(rank ^ 2, T.h1p, T.h1, halves("ah1")[0], on)])
+        to = [(helper(rank), T.ph, names("aph")), (helper(rank ^ 2), T.php, names("aphp"))]
+        engs = deal([d for d, _, _ in to])
+        for k in alone:
+            write([(names("r0")[k], 1)], [(d, buf[:, col(k)], T.h1[:, col(k)], arr[k], engs[d]) for d, buf, arr in to])
+        to = [(d, buf, arr, k_help) for d, buf, arr in to]
+        to += [(cores[mine], T.ph, names("aph"), k_carr), (cores[carrier(rank ^ 2)], T.php, names("aphp"), k_carr)]
+        engs = deal([d for d, _, _, _ in to])
+        write(ones(names("r0"), PIECES[-1]),
+              [(d, buf[:, col(k)], T.h1[:, col(k)], arr[k], engs[d]) for d, buf, arr, k in to])
+        write([], [(cores[rank ^ 2], T.h1p[:], T.h1[:], names("ah1")[0], on)])
     else:
-        for j in range(NP):
-            send(j, ones(names("r0"), quarters(j)), [(rank ^ 2, T.h1p, T.h1, halves("ah1")[j], far)])
-    product(high, T.ws[:, 256:384], T.h1, ones(names("r0")) + [(sem.ldw12, 16)], every, True)
-    for j in range(NP):
-        landed = (halves("ah1")[0], len(on)) if mine != rank else (halves("ah1")[j], len(far))
-        product(high, T.ws[:, 384:512], T.h1p, [landed], quarters(j), False, names("m1"))
-        relu(T.h2, high, names("m1"), names("r1"), quarters(j))
-        if client is not None:
-            for k in quarters(j):
-                product(low, T.pw[:, 0:128], T.ph, [(sem.apw, len(rest)), (halves("aph")[j], len(on) // 2)], [k], True)
-                product(low, T.pw[:, 128:256], T.php, [(halves("aphp")[j], len(on) // 2)], [k], False, names("mp"))
-            relu(T.ph2, low, names("mp"), names("rp"), quarters(j))
+        for j, ks in enumerate(PIECES):
+            write(ones(names("r0"), ks), [(cores[rank ^ 2], T.h1p[:, span(ks)], T.h1[:, span(ks)], names("ah1")[j], far)])
+    product(high, T.ws[:, 256:384], T.h1, ones(names("r0")) + [(sem.ldw1, 16)], every, True)
+    for j, ks in enumerate(PIECES):
+        landed = (names("ah1")[0], len(on)) if mine != rank else (names("ah1")[j], len(far))
+        product(high, T.ws[:, 384:512], T.h1p, [landed], ks, False, names("m1"))
+        relu(T.h2, high, names("m1"), names("r1"), ks)
+    if client is not None:
+        second_layer1(k_carr, len(far), len(on) // 4)
 
     if mine == rank:
-        for j in range(NP):
-            send(j, ones(names("r1"), quarters(j)), [(rank ^ 4, T.h2p, T.h2, halves("ah2")[j], far)])
-            if client is not None:
-                send(j, ones(names("rp"), quarters(j)), [(client ^ 4, T.h2p, T.ph2, halves("ah2")[j], far)])
-    product(high, T.ws[:, 512:640], T.h2, ones(names("r1")) + [(sem.ldw12, 16)], every, True)
-    for j in range(NP):
-        product(high, T.ws[:, 640:768], T.h2p, [(halves("ah2")[j], len(far))], quarters(j), False, names("m2"))
+        for j, ks in enumerate(PIECES):
+            write(ones(names("r1"), ks), [(cores[rank ^ 4], T.h2p[:, span(ks)], T.h2[:, span(ks)], names("ah2")[j], far)])
+        if client is not None:
+            k = k_carr
+            write([(names("rp")[k], 1)], [(cores[client ^ 4], T.h2p[:, col(k)], T.ph2[:, col(k)], names("ah2")[k], far)])
+    product(high, T.ws[:, 512:640], T.h2, ones(names("r1")) + [(sem.ldw2, 16)], every, True)
+    arrivals = list(enumerate(PIECES)) if mine == rank else [(k, (k,)) for k in every]
+    for j, ks in arrivals:
+        product(high, T.ws[:, 640:768], T.h2p, [(names("ah2")[j], len(far))], ks, False, names("m2"))
     relu(T.ys, high, names("m2"), names("r2"), every)
 
-    for j, q in zip(range(NP), (g.sync, g.scalar)):
-        for s, v in ones(names("r2"), quarters(j)):
+    plan = [(g.sync, (0, 1)), (g.scalar, (2,)), (g.sync, (3,))]
+    for i, (q, ks) in enumerate(plan):
+        for s, v in ones(names("r2"), ks):
             q.wait_ge(s, v)
-        q.dma_start(T.y[:, half(j)], T.ys[:, half(j)]).then_inc(halves("st")[j], 16)
-        q.wait_ge(halves("st")[j], 16)
+        q.dma_start(T.y[:, span(ks)], T.ys[:, span(ks)]).then_inc(names("st")[i], 16)
+    for i, (q, ks) in enumerate(plan):
+        q.wait_ge(names("st")[i], 16)
     g.wait_ge(sem.sent, sent[0])

from concourse.bass import DstId, RemoteDMATransfer
from concourse.mybir import AluOpType

NCORES = 64
TK = 512
KC = 4
W = TK // KC
PIECES = ((0,), (1,), (2, 3))
BF, F32 = "bfloat16", "float32"

SCRATCH = {
    "xs": ("sbuf", [128, TK], BF),
    "ws": ("sbuf", [128, 768], BF),
    "xp": ("sbuf", [128, TK], BF),
    "h1": ("sbuf", [128, TK], BF),
    "h1p": ("sbuf", [128, TK], BF),
    "pw": ("sbuf", [128, 256], BF),
    "ph": ("sbuf", [128, TK], BF),
    "php": ("sbuf", [128, TK], BF),
    "h2": ("sbuf", [128, TK], BF),
    "ph2": ("sbuf", [128, TK], BF),
    "h2p": ("sbuf", [128, TK], BF),
    "ys": ("sbuf", [128, TK], BF),
    "zero": ("sbuf", [128, W], F32),
}
for _k in range(2 * KC):
    SCRATCH["bank_%d" % _k] = ("psum", [128, 512], F32)

SEMAPHORES = ["ldw0", "ldw1", "ldw2", "zs", "apw", "sent"]
for _n in ("ldx", "ax", "aph", "aphp", "ah1", "ah2", "st", "m0", "m1", "mp", "m2", "r0", "r1", "rp", "r2"):
    for _k in range(KC):
        SEMAPHORES.append("%s_%d" % (_n, _k))


def rank_program(g, core, T, topo):
    rank = T.rank_of(core)
    cores = T.cores
    n = len(cores)
    sem = T.sem

    def carrier(r):
        dst = cores[r ^ 4]
        if topo.may_write(cores[r], dst):
            return r
        cand = [q for q in range(n) if q != r and topo.chip(cores[q]) == topo.chip(cores[r])
                and topo.may_write(cores[q], dst) and topo.may_write(cores[q], cores[q ^ 4])]
        cand.sort(key=lambda q: (topo.die(cores[q]) != topo.die(cores[r]), abs(q - r)))
        return cand[0]

    def helper(r):
        cand = [c for c in range(NCORES) if c not in cores and topo.chip(c) == topo.chip(cores[r])
                and topo.may_write(c, cores[r ^ 4])]
        cand.sort(key=lambda c: (topo.die(c) != topo.die(cores[r]), c))
        return cand[0]

    served = None
    if rank is None:
        mineq = [r for r in range(n) if carrier(r) != r and helper(r) == core]
        if not mineq:
            return
        served = mineq[0]

    def bits(m):
        return [b for b in range(m.bit_length()) if (m >> b) & 1]

    def to_mask(bs):
        m = 0
        for b in bs:
            m |= 1 << b
        return m

    base = served if rank is None else rank
    on = bits(topo.mask(core, cores[base] if rank is None else cores[base ^ 1]))
    far = bits(topo.mask(core, cores[base ^ 4]))
    rest = [b for b in on if b not in far]
    sent = [0]

    def col(k):
        return slice(k * W, (k + 1) * W)

    def span(ks):
        return slice(ks[0] * W, (ks[-1] + 1) * W)

    def names(stem):
        return [sem["%s_%d" % (stem, k)] for k in range(KC)]

    def banks(first):
        return [T["bank_%d" % (first + k)] for k in range(KC)]

    low, high = banks(0), banks(KC)

    def write(waits, dests):
        for s, v in waits:
            g.wait_ge(s, v)
        trs = []
        for dst, out, src, arr, engs in dests:
            rid, pid, _ = topo.addr(dst)
            sent[0] += len(engs)
            if len(dests) == 1:
                g.remote_dma(out_ap=out, in_ap=src, remote_sem=arr, local_sem=sem.sent, pid=pid,
                             routing_id=rid, dma_engine_mask=to_mask(engs))
            else:
                trs.append(RemoteDMATransfer(dst_ids=[DstId(rid=rid, pnc=pid)], dma_engine_mask=to_mask(engs),
                                             remote_sem=arr, src=src, dst=out))
        if trs:
            g.remote_dma_fused(trs, local_sem=sem.sent)

    def deal(dsts):
        cross = [d for d in dsts if topo.die(d) != topo.die(core)]
        stay = [d for d in dsts if d not in cross]
        pools = ((cross, on[0::2]), (stay, on[1::2])) if len(cross) == len(stay) else ((dsts, on),)
        out = {}
        for grp, pool in pools:
            for i, d in enumerate(grp):
                out[d] = pool[i::len(grp)]
        return out

    def product(acc, wt, h, waits, ks, first, done=None):
        for s, v in waits:
            g.tensor.wait_ge(s, v)
        for k in ks:
            mm = g.tensor.matmul(acc[k][:, 0:W], wt, h[:, col(k)], first, done is not None)
            if done is not None:
                mm.then_inc(done[k], 1)

    def relu(out, acc, done, ready, ks):
        for k in ks:
            g.vector.wait_ge(done[k], 1)
            g.vector.tensor_tensor(out[:, col(k)], acc[k][:, 0:W], T.zero[:], AluOpType.max).then_inc(ready[k], 1)

    def ones(sems, ks=range(KC)):
        return [(sems[k], 1) for k in ks]

    def second_layer1(k, npw, cnt):
        product(low, T.pw[:, 0:128], T.ph, [(sem.apw, npw), (names("aph")[k], cnt)], [k], True)
        product(low, T.pw[:, 128:256], T.php, [(names("aphp")[k], cnt)], [k], False, names("mp"))
        relu(T.ph2, low, names("mp"), names("rp"), [k])

    every = list(range(KC))
    alone = [p[0] for p in PIECES if len(p) == 1]
    k_help, k_carr = PIECES[-1]
    g.vector.memset(T.zero[:], 0.0).then_inc(sem.zs, 1)
    g.vector.wait_ge(sem.zs, 1)

    if rank is None:
        write([(sem.apw, len(rest))], [(cores[carrier(served)], T.pw[:], T.pw[:], sem.apw, far)])
        for k in alone + [k_help]:
            second_layer1(k, len(rest), len(on) // 2 if k in alone else len(on) // 4)
            write([(names("rp")[k], 1)], [(cores[served ^ 4], T.h2p[:, col(k)], T.ph2[:, col(k)], names("ah2")[k], far)])
        g.wait_ge(sem.sent, sent[0])
        return

    mine = carrier(rank)
    clients = [r for r in range(n) if r != rank and carrier(r) == rank]
    client = clients[0] if clients else None
    npc = len(PIECES)

    for j, ks in enumerate(PIECES):
        g.sync.dma_start(T.xs[:, span(ks)], T.x[:, span(ks)]).then_inc(names("ldx")[j], 16)
    for l in ((1, 0, 2) if mine != rank else (0, 1, 2)):
        g.sync.dma_start(T.ws[:, 256 * l:256 * l + 256], T.w[:, 256 * l:256 * l + 256]).then_inc(sem["ldw%d" % l], 16)

    for j, ks in enumerate(PIECES):
        write([(names("ldx")[j], 16)], [(cores[rank ^ 1], T.xp[:, span(ks)], T.xs[:, span(ks)], names("ax")[j], far)])
    if mine != rank:
        write([(sem.ldw1, 16)], [(helper(rank), T.pw[:], T.ws[:, 256:512], sem.apw, rest)])
    product(low, T.ws[:, 0:128], T.xs, [(names("ldx")[j], 16) for j in range(npc)] + [(sem.ldw0, 16)], every, True)
    for j, ks in enumerate(PIECES):
        product(low, T.ws[:, 128:256], T.xp, [(names("ax")[j], len(far))], ks, False, names("m0"))
    relu(T.h1, low, names("m0"), names("r0"), every)

    if mine != rank:
        to = [(helper(rank), T.ph, names("aph")), (helper(rank ^ 2), T.php, names("aphp"))]
        engs = deal([d for d, _, _ in to])
        for k in alone:
            write([(names("r0")[k], 1)], [(d, buf[:, col(k)], T.h1[:, col(k)], arr[k], engs[d]) for d, buf, arr in to])
        to = [(d, buf, arr, k_help) for d, buf, arr in to]
        to += [(cores[mine], T.ph, names("aph"), k_carr), (cores[carrier(rank ^ 2)], T.php, names("aphp"), k_carr)]
        engs = deal([d for d, _, _, _ in to])
        write(ones(names("r0"), PIECES[-1]),
              [(d, buf[:, col(k)], T.h1[:, col(k)], arr[k], engs[d]) for d, buf, arr, k in to])
        write([], [(cores[rank ^ 2], T.h1p[:], T.h1[:], names("ah1")[0], on)])
    else:
        for j, ks in enumerate(PIECES):
            write(ones(names("r0"), ks), [(cores[rank ^ 2], T.h1p[:, span(ks)], T.h1[:, span(ks)], names("ah1")[j], far)])
    product(high, T.ws[:, 256:384], T.h1, ones(names("r0")) + [(sem.ldw1, 16)], every, True)
    for j, ks in enumerate(PIECES):
        landed = (names("ah1")[0], len(on)) if mine != rank else (names("ah1")[j], len(far))
        product(high, T.ws[:, 384:512], T.h1p, [landed], ks, False, names("m1"))
        relu(T.h2, high, names("m1"), names("r1"), ks)
    if client is not None:
        second_layer1(k_carr, len(far), len(on) // 4)

    if mine == rank:
        for j, ks in enumerate(PIECES):
            write(ones(names("r1"), ks), [(cores[rank ^ 4], T.h2p[:, span(ks)], T.h2[:, span(ks)], names("ah2")[j], far)])
        if client is not None:
            k = k_carr
            write([(names("rp")[k], 1)], [(cores[client ^ 4], T.h2p[:, col(k)], T.ph2[:, col(k)], names("ah2")[k], far)])
    product(high, T.ws[:, 512:640], T.h2, ones(names("r1")) + [(sem.ldw2, 16)], every, True)
    arrivals = list(enumerate(PIECES)) if mine == rank else [(k, (k,)) for k in every]
    for j, ks in arrivals:
        product(high, T.ws[:, 640:768], T.h2p, [(names("ah2")[j], len(far))], ks, False, names("m2"))
    relu(T.ys, high, names("m2"), names("r2"), every)

    plan = [(g.sync, (0, 1)), (g.scalar, (2,)), (g.sync, (3,))]
    for i, (q, ks) in enumerate(plan):
        for s, v in ones(names("r2"), ks):
            q.wait_ge(s, v)
        q.dma_start(T.y[:, span(ks)], T.ys[:, span(ks)]).then_inc(names("st")[i], 16)
    for i, (q, ks) in enumerate(plan):
        q.wait_ge(names("st")[i], 16)
    g.wait_ge(sem.sent, sent[0])
